import numpy as np, ml_dtypes
CORES = [2,6,26,30,66,70,74,78,82,86]
N = 10
GR, GC = 5, 2
L, KA, KB, F = 20, 10, 4, 64
def setup_inputs(rng):
    return {"a": rng.standard_normal((N, 128, KA * 128), dtype=np.float32).astype(ml_dtypes.bfloat16), "b": rng.standard_normal((N, 128, KB * F), dtype=np.float32).astype(ml_dtypes.bfloat16)}
def reference(a, b):
    A, B = a.astype(np.float64), b.astype(np.float64)
    y = np.zeros((N, 128, F))
    for i in range(GR):
        for j in range(GC):
            for k in range(L):
                At = A[i * GC + k // KA][:, 128 * (k % KA):128 * (k % KA) + 128]
                Bt = B[(k // KB) * GC + j][:, F * (k % KB):F * (k % KB) + F]
                y[i * GC + j] += At.T @ Bt
    return {"y": y.astype(ml_dtypes.bfloat16 if a.dtype != np.float64 else np.float64)}

from concourse.bass import DstId, RemoteDMATransfer

GR, GC = 5, 2
L, KA, KB, F = 20, 10, 4, 64
P = 128
BW = KB * F

SCRATCH = {
    "a_own": ("sbuf", [P, KA * P], "bfloat16"),
    "a_mate": ("sbuf", [P, KA * P], "bfloat16"),
    "b_all": ("sbuf", [P, GR * BW], "bfloat16"),
    "y_sb": ("sbuf", [P, F], "bfloat16"),
    "acc": ("psum", [P, F], "float32"),
}
SEMAPHORES = ["b_ld", "a_ld", "a_in", "sent", "mm", "cp", "st"] + ["b_in%d" % r for r in range(GR)]


def _count(mask):
    return bin(mask).count("1")


def rank_program(g, core, T, topo):
    rank = T.rank_of(core)
    if rank is None:
        return
    i, j = divmod(rank, GC)
    sem = T.sem
    mate = T.cores[i * GC + (1 - j)]
    own_b = T.b_all[:, i * BW:(i + 1) * BW]
    H = P // 2

    for q, lo in ((g.sync, 0), (g.scalar, H)):
        q.dma_start(T.b_all[lo:lo + H, i * BW:(i + 1) * BW], T.b[lo:lo + H, :]).then_inc(sem.b_ld, 16)
        q.dma_start(T.a_own[lo:lo + H, :], T.a[lo:lo + H, :]).then_inc(sem.a_ld, 16)

    dests = [T.cores[((i + s) % GR) * GC + j] for s in range(1, GR)]
    off = topo.mask(core, mate)
    for d in dests:
        assert topo.may_write(core, d)
        off &= topo.mask(core, d)
    g.wait_ge(sem.b_ld, 32)
    g.remote_dma_fused(
        [RemoteDMATransfer(
            dst_ids=[DstId(rid=topo.addr(d)[0], pnc=topo.addr(d)[1]) for d in dests],
            dma_engine_mask=off, remote_sem=sem["b_in%d" % i],
            srcs=[own_b], dsts=[own_b for _ in dests], alu_op=0)],
        local_sem=sem.sent)

    on = topo.mask(core, mate) & ~off
    rid, pid, _ = topo.addr(mate)
    g.wait_ge(sem.a_ld, 32)
    g.remote_dma(T.a_mate[:, :], T.a_own[:, :], sem.a_in, sem.sent, pid, rid, on)

    def when(k):
        tb = (i - k // KB) % GR
        ta = 0.0 if k // KA == j else 3.5
        return (max(tb, ta), tb, k)

    waited = set()

    def need(name, val):
        if name not in waited:
            waited.add(name)
            g.tensor.wait_ge(sem[name], val)

    mm = None
    order = sorted(range(L), key=when)
    for n, k in enumerate(order):
        r = k // KB
        if r == i:
            need("b_ld", 32)
        else:
            need("b_in%d" % r, _count(off))
        if k // KA == j:
            need("a_ld", 32)
            src = T.a_own
        else:
            need("a_in", _count(on))
            src = T.a_mate
        t = k % KA
        mm = g.tensor.matmul(T.acc[:, :], src[:, t * P:(t + 1) * P], T.b_all[:, k * F:(k + 1) * F],
                             n == 0, n == L - 1)
    mm.then_inc(sem.mm, 1)

    g.vector.wait_ge(sem.mm, 1)
    g.vector.tensor_copy(T.y_sb[:, :], T.acc[:, :]).then_inc(sem.cp, 1)
    g.sync.wait_ge(sem.cp, 1)
    g.sync.dma_start(T.y[:, :], T.y_sb[:, :]).then_inc(sem.st, 16)
    g.sync.wait_ge(sem.st, 16)
    g.wait_ge(sem.sent, _count(off) + _count(on))
